import numpy as np
import ml_dtypes


def mxq(x, axis, fmt="e4m3"):
    dtype, down = {"e4m3": (ml_dtypes.float8_e4m3fn, 7), "e5m2": (ml_dtypes.float8_e5m2, 14)}[fmt]
    v = np.moveaxis(np.asarray(x, np.float32).astype(ml_dtypes.bfloat16).astype(np.float64), axis, -1)
    blocks = v.reshape(v.shape[:-1] + (-1, 32))
    amax = np.abs(blocks).max(-1, keepdims=True)
    byte = np.maximum(np.where(amax > 0, np.frexp(amax)[1] - 1 + 127, 0) - down, 1)
    scale = np.exp2(byte - 127.0)
    codes = (blocks / scale).astype(np.float32).astype(dtype).astype(np.float64)
    return np.moveaxis((codes * scale).reshape(v.shape), -1, axis)


WIDE = False


def mx_kscale(k):
    if not WIDE:
        return np.ones(k)
    levels = np.array([10, -10, 5, -5, 0])
    if k % 512:
        return np.exp2(np.random.permutation(np.resize(levels, k // 32))).repeat(32)
    a = np.empty((k // 512, 16))
    for p in range(k // 512):
        a[p, :8] = np.random.permutation(np.resize(levels, 8))
        for g in range(8):
            far = levels[np.abs(levels - a[p, g]) >= 10]
            a[p, g + 8] = far[np.random.randint(len(far))]
    return np.exp2(a.ravel()).repeat(32)


def f64(x):
    return np.asarray(x).astype(np.float64)


def striped(idx):
    return np.tile(np.asarray(idx).reshape(-1, 16).T, (8, 1)).astype(np.uint16)


def unstriped(offs):
    return offs[:16].T.reshape(-1).astype(np.int64)


E2M1 = np.array([0.0, 0.5, 1.0, 1.5, 2.0, 3.0, 4.0, 6.0, -0.0, -0.5, -1.0, -1.5, -2.0, -3.0, -4.0, -6.0])


def pack_weight(w, fmt):
    k, n = w.shape
    w = f64(np.asarray(w, np.float32).astype(ml_dtypes.bfloat16)).reshape(k // 32, 32, n)
    amax = np.abs(w).max(1)
    if fmt == "e4m3":
        byte = np.frexp(amax)[1] - 1 + 127 - 7
    else:
        mant, ex = np.frexp(amax / 6.0)
        byte = np.where(mant > 0.5, ex, ex - 1) + 127
    byte = np.clip(np.where(amax > 0, byte, 1), 1, 254)
    scaled = (w * np.exp2(127.0 - byte)[:, None, :]).reshape(k, n).astype(np.float32)
    by_word = np.ascontiguousarray(scaled.reshape(k // 512, 128, 4, n).transpose(0, 1, 3, 2))
    if fmt == "e4m3":
        words = by_word.astype(ml_dtypes.float8_e4m3fn).view(np.uint8)
    else:
        c = by_word.astype(ml_dtypes.float4_e2m1fn).view(np.uint8) & 0xF
        words = (c[..., 0::2] | (c[..., 1::2] << 4)).reshape(k // 512, 128, 2 * n)
    return np.ascontiguousarray(words), np.ascontiguousarray(byte.astype(np.uint8).reshape(k // 512, 16, n))


def unpack_weight(words, scales, fmt):
    g, _, n = scales.shape
    words = np.ascontiguousarray(words).reshape(g, 128, n, -1)
    if fmt == "e4m3":
        vals = words.view(ml_dtypes.float8_e4m3fn).astype(np.float64)
    else:
        nib = np.empty((g, 128, n, 4), np.uint8)
        nib[..., 0::2] = words & 0xF
        nib[..., 1::2] = words >> 4
        vals = E2M1[nib]
    vals = vals * np.repeat(np.exp2(scales.astype(np.float64) - 127.0), 8, axis=1)[..., None]
    return vals.transpose(0, 1, 3, 2).reshape(g * 512, n)


B, N, T, D, NQ = 1, 512, 2048, 512, 128


def setup_inputs():
    n = np.random.standard_normal
    idx = np.random.permutation(T)[:B * N]
    s = mx_kscale(D)[:, None]
    kp = pack_weight(n((D, T)) / s, "e4m3")
    return {
        "qT": (n((B, D, NQ)) * s * (0.50 / np.sqrt(D))).astype(np.float32),
        "k_words": kp[0],
        "k_scales": kp[1],
        "kn": np.tile(np.random.uniform(1.0, 4.0, 2048), (128, 1)).astype(np.float32),
        "qn": (np.random.uniform(1.0, 4.0, (B, NQ, 1))).astype(np.float32),
        "offs": striped(idx),
    }


def reference(qT, k_words, k_scales, kn, qn, offs):
    idx = unstriped(offs)
    pick = lambda x, which: x[:, which].reshape(x.shape[0], B, -1).transpose(1, 0, 2)
    k = unpack_weight(k_words, k_scales, "e4m3")
    kg = pick(k, idx)
    qq = mxq(f64(qT), 1, "e4m3")
    a = qq.transpose(0, 2, 1) @ kg
    t = 1.0 / (1.0 + np.maximum(f64(qn) + pick(f64(kn), idx)[:, :1, :] - 2.0 * a, 0.0))
    y = t / np.sum(t, axis=-1, keepdims=True)
    return y

@@ -1,0 +1,138 @@
+from contextlib import ExitStack
+
+import concourse.mybir as mybir
+from concourse.masks import make_identity
+
+F32 = mybir.dt.float32
+BF16 = mybir.dt.bfloat16
+I32 = mybir.dt.int32
+U32 = mybir.dt.uint32
+U16 = mybir.dt.uint16
+U8 = mybir.dt.uint8
+FP8X4 = mybir.dt.float8_e4m3fn_x4
+ACT = mybir.ActivationFunctionType
+ALU = mybir.AluOpType
+
+P = 128
+PACK = 4
+T = 2048
+N = 512
+NQ = 128
+HALF = N // 2
+KN_ROW = P - 1
+
+FLOPS = 2 * NQ * N * P * PACK
+
+
+def tile_attend_student_topk_kernel(tc, qT, k_words, k_scales, kn, qn, offs, out):
+    nc = tc.nc
+    with ExitStack() as ctx:
+        sb = ctx.enter_context(tc.tile_pool(name="sb", bufs=1))
+        ps = ctx.enter_context(tc.psum_pool(name="ps", bufs=1))
+
+        offsets = sb.tile([P, N // 16], U16, name="offsets")
+        scale_tab = sb.tile([P, T // 4], I32, name="scale_tab", align_bytes=64)
+        kn_tab = sb.tile([P, T], F32, name="kn_tab", align_bytes=64)
+        word_tab = sb.tile([P, T], I32, name="word_tab", align_bytes=64)
+        q_raw = sb.tile([P, PACK, NQ], F32, name="q_raw", align_bytes=64)
+        qn_col = sb.tile([P, 1], F32, name="qn_col")
+        ident = sb.tile([P, P], F32, name="ident", align_bytes=64)
+
+        nc.vector.memset(scale_tab[:], 0)
+        nc.vector.memset(kn_tab[0:KN_ROW, :], 0.0)
+
+        nc.sync.dma_start(offsets[:], offs)
+        nc.sync.dma_start(kn_tab[KN_ROW:P, :], kn[0:1, :])
+        for quad in range(4):
+            nc.scalar.dma_start(
+                scale_tab[32 * quad : 32 * quad + 4, :],
+                k_scales[0, 4 * quad : 4 * quad + 4, :].bitcast(I32),
+            )
+        nc.sync.dma_start(q_raw[:], qT[0].rearrange("(p j) w -> p j w", j=PACK))
+        nc.sync.dma_start(word_tab[:], k_words[0].rearrange("p n t -> p (n t)").bitcast(I32))
+        make_identity(nc, ident[:])
+        nc.gpsimd.dma_start(qn_col[:], qn[0])
+
+        kn_row = sb.tile([P, N], F32, name="kn_row", align_bytes=64)
+        nc.vector.tensor_copy(kn_row[:], kn_tab[:].indirect(offsets[:]))
+
+        k_sc = sb.tile([P, N], U8, name="k_sc", align_bytes=64)
+        nc.vector.tensor_copy(k_sc[:], scale_tab[:].bitcast(U8).indirect(offsets[:]))
+
+        q_bf = sb.tile([P, NQ, PACK], BF16, name="q_bf", align_bytes=64)
+        nc.scalar.copy(q_bf[:], q_raw[:].rearrange("p j w -> p w j"))
+        q_codes = sb.tile([P, NQ], U32, name="q_codes", align_bytes=64)
+        q_sc = sb.tile([P, NQ], U8, name="q_sc", align_bytes=64)
+        nc.vector.quantize_mx(
+            out=q_codes[:].bitcast(FP8X4),
+            scales=q_sc[:],
+            in_=q_bf[:].rearrange("p w j -> p (w j)"),
+        )
+
+        kn_turned = ps.tile([P, N // P, P], F32, name="kn_turned")
+        for j in range(N // P):
+            nc.tensor.transpose(kn_turned[:, j, :], kn_row[:, j * P : (j + 1) * P], ident[:])
+        kn_cols = sb.tile([P, N // P], F32, name="kn_cols")
+        nc.scalar.copy(kn_cols[:], kn_turned[:, :, KN_ROW])
+        kn_spread = ps.tile([P, N], F32, name="kn_spread")
+        for j in range(N // P):
+            nc.tensor.transpose(
+                kn_spread[:, j * P : (j + 1) * P],
+                kn_cols[:, j : j + 1].to_broadcast([P, P]),
+                ident[:],
+            )
+        kn_all = sb.tile([P, N], F32, name="kn_all", align_bytes=64)
+        nc.scalar.copy(kn_all[:], kn_spread[:])
+
+        dots = []
+        for h in range(2):
+            k_codes = sb.tile([P, HALF], U32, name="k_codes%d" % h, align_bytes=64)
+            cols = slice(h * HALF // 16, (h + 1) * HALF // 16)
+            nc.vector.tensor_copy(k_codes[:], word_tab[:].bitcast(U32).indirect(offsets[:, cols]))
+            dot = ps.tile([P, HALF], F32, name="dot%d" % h)
+            nc.tensor.matmul_mx(
+                out=dot[:],
+                lhsT=q_codes[:].bitcast(FP8X4),
+                lhsT_scale=q_sc[:],
+                rhs=k_codes[:].bitcast(FP8X4),
+                rhs_scale=k_sc[:, h * HALF : (h + 1) * HALF],
+                start=True,
+                stop=True,
+            )
+            dots.append(dot)
+
+        roots = []
+        sims = []
+        sums = []
+        for h in range(2):
+            part = sb.tile([P, HALF], F32, name="part%d" % h, align_bytes=64)
+            nc.vector.scalar_tensor_tensor(
+                part[:], dots[h][:], -2.0, kn_all[:, h * HALF : (h + 1) * HALF], ALU.mult, ALU.add
+            )
+            dist = sb.tile([P, HALF], F32, name="dist%d" % h, align_bytes=64)
+            if h == 0:
+                nc.scalar.activation(dist[:], part[:], ACT.Relu, bias=qn_col[:])
+            else:
+                nc.vector.tensor_scalar(dist[:], part[:], qn_col[:], 0.0, ALU.add, ALU.max)
+            root = sb.tile([P, HALF], F32, name="root%d" % h, align_bytes=64)
+            nc.scalar.activation(root[:], dist[:], ACT.Abs_reciprocal_sqrt, bias=1.0)
+            sim = sb.tile([P, HALF], F32, name="sim%d" % h, align_bytes=64)
+            total = sb.tile([P, 1], F32, name="total%d" % h)
+            if h == 0:
+                nc.vector.scalar_tensor_tensor(
+                    sim[:], root[:], 1.0, root[:], ALU.mult, ALU.mult, accum_out=total[:]
+                )
+            else:
+                nc.scalar.activation(sim[:], root[:], ACT.Square, accum_out=total[:])
+            roots.append(root)
+            sims.append(sim)
+            sums.append(total)
+
+        norm = sb.tile([P, 1], F32, name="norm")
+        nc.scalar.activation(norm[:], sums[1][:], ACT.Abs_reciprocal_sqrt, bias=sums[0][:])
+        res0 = sb.tile([P, HALF], F32, name="res0", align_bytes=64)
+        nc.vector.tensor_scalar(res0[:], sims[0][:], norm[:], norm[:], ALU.mult, ALU.mult)
+        nc.sync.dma_start(out[0, :, 0:HALF], res0[:])
+        res1 = sb.tile([P, HALF], F32, name="res1", align_bytes=64)
+        nc.scalar.activation(res1[:], roots[1][:], ACT.Square, scale=norm[:])
+        nc.scalar.dma_start(out[0, :, HALF:N], res1[:])

@@ -32,7 +32,7 @@ def tile_attend_student_topk_kernel(tc, qT, k_words, k_scales, kn, qn, offs, out
 
         offsets = sb.tile([P, N // 16], U16, name="offsets")
         scale_tab = sb.tile([P, T // 4], I32, name="scale_tab", align_bytes=64)
-        kn_tab = sb.tile([P, T], F32, name="kn_tab", align_bytes=64)
+        kn_tab = sb.tile([P, T], F32, name="kn_tab", tag="shared", align_bytes=64)
         word_tab = sb.tile([P, T], I32, name="word_tab", align_bytes=64)
         q_raw = sb.tile([P, PACK, NQ], F32, name="q_raw", align_bytes=64)
         qn_col = sb.tile([P, 1], F32, name="qn_col")
@@ -43,20 +43,28 @@ def tile_attend_student_topk_kernel(tc, qT, k_words, k_scales, kn, qn, offs, out
 
         nc.sync.dma_start(offsets[:], offs)
         nc.sync.dma_start(kn_tab[KN_ROW:P, :], kn[0:1, :])
+        nc.sync.dma_start(q_raw[:], qT[0].rearrange("(p j) w -> p j w", j=PACK))
         for quad in range(4):
-            nc.scalar.dma_start(
+            nc.sync.dma_start(
                 scale_tab[32 * quad : 32 * quad + 4, :],
                 k_scales[0, 4 * quad : 4 * quad + 4, :].bitcast(I32),
             )
-        nc.sync.dma_start(q_raw[:], qT[0].rearrange("(p j) w -> p j w", j=PACK))
         nc.sync.dma_start(word_tab[:], k_words[0].rearrange("p n t -> p (n t)").bitcast(I32))
+        warm = sb.tile([P, 1], F32, name="warm")
+        nc.scalar.activation(warm[0:KN_ROW, :], kn_tab[0:KN_ROW, 0:1], ACT.Abs_reciprocal_sqrt, bias=1.0)
         make_identity(nc, ident[:])
-        nc.gpsimd.dma_start(qn_col[:], qn[0])
+        nc.sync.dma_start(qn_col[:], qn[0])
 
-        kn_row = sb.tile([P, N], F32, name="kn_row", align_bytes=64)
-        nc.vector.tensor_copy(kn_row[:], kn_tab[:].indirect(offsets[:]))
+        def half_offsets(h):
+            return offsets[:, h * HALF // 16 : (h + 1) * HALF // 16]
 
-        k_sc = sb.tile([P, N], U8, name="k_sc", align_bytes=64)
+        kn_rows = []
+        for h in range(2):
+            kn_row = sb.tile([P, HALF], F32, name="kn_row%d" % h, align_bytes=64)
+            nc.vector.tensor_copy(kn_row[:], kn_tab[:].indirect(half_offsets(h)))
+            kn_rows.append(kn_row)
+
+        k_sc = sb.tile([P, N], U8, name="k_sc", tag="shared", align_bytes=64)
         nc.vector.tensor_copy(k_sc[:], scale_tab[:].bitcast(U8).indirect(offsets[:]))
 
         q_bf = sb.tile([P, NQ, PACK], BF16, name="q_bf", align_bytes=64)
@@ -69,26 +77,31 @@ def tile_attend_student_topk_kernel(tc, qT, k_words, k_scales, kn, qn, offs, out
             in_=q_bf[:].rearrange("p w j -> p (w j)"),
         )
 
-        kn_turned = ps.tile([P, N // P, P], F32, name="kn_turned")
-        for j in range(N // P):
-            nc.tensor.transpose(kn_turned[:, j, :], kn_row[:, j * P : (j + 1) * P], ident[:])
-        kn_cols = sb.tile([P, N // P], F32, name="kn_cols")
-        nc.scalar.copy(kn_cols[:], kn_turned[:, :, KN_ROW])
-        kn_spread = ps.tile([P, N], F32, name="kn_spread")
-        for j in range(N // P):
-            nc.tensor.transpose(
-                kn_spread[:, j * P : (j + 1) * P],
-                kn_cols[:, j : j + 1].to_broadcast([P, P]),
-                ident[:],
-            )
-        kn_all = sb.tile([P, N], F32, name="kn_all", align_bytes=64)
-        nc.scalar.copy(kn_all[:], kn_spread[:])
+        kn_colss = []
+        for h in range(2):
+            kn_turned = ps.tile([P, 2, P], F32, name="kn_turned%d" % h)
+            for j in range(2):
+                nc.tensor.transpose(kn_turned[:, j, :], kn_rows[h][:, j * P : (j + 1) * P], ident[:])
+            kn_cols = sb.tile([P, 2], F32, name="kn_cols%d" % h)
+            nc.scalar.copy(kn_cols[:], kn_turned[:, :, KN_ROW])
+            kn_colss.append(kn_cols)
+        kn_alls = []
+        for h in range(2):
+            kn_spread = ps.tile([P, HALF], F32, name="kn_spread%d" % h)
+            for j in range(2):
+                nc.tensor.transpose(
+                    kn_spread[:, j * P : (j + 1) * P],
+                    kn_colss[h][:, j : j + 1].to_broadcast([P, P]),
+                    ident[:],
+                )
+            kn_all = sb.tile([P, HALF], F32, name="kn_all%d" % h, align_bytes=64)
+            nc.scalar.copy(kn_all[:], kn_spread[:])
+            kn_alls.append(kn_all)
 
         dots = []
         for h in range(2):
             k_codes = sb.tile([P, HALF], U32, name="k_codes%d" % h, align_bytes=64)
-            cols = slice(h * HALF // 16, (h + 1) * HALF // 16)
-            nc.vector.tensor_copy(k_codes[:], word_tab[:].bitcast(U32).indirect(offsets[:, cols]))
+            nc.vector.tensor_copy(k_codes[:], word_tab[:].bitcast(U32).indirect(half_offsets(h)))
             dot = ps.tile([P, HALF], F32, name="dot%d" % h)
             nc.tensor.matmul_mx(
                 out=dot[:],
@@ -106,9 +119,7 @@ def tile_attend_student_topk_kernel(tc, qT, k_words, k_scales, kn, qn, offs, out
         sums = []
         for h in range(2):
             part = sb.tile([P, HALF], F32, name="part%d" % h, align_bytes=64)
-            nc.vector.scalar_tensor_tensor(
-                part[:], dots[h][:], -2.0, kn_all[:, h * HALF : (h + 1) * HALF], ALU.mult, ALU.add
-            )
+            nc.vector.scalar_tensor_tensor(part[:], dots[h][:], -2.0, kn_alls[h][:], ALU.mult, ALU.add)
             dist = sb.tile([P, HALF], F32, name="dist%d" % h, align_bytes=64)
             if h == 0:
                 nc.scalar.activation(dist[:], part[:], ACT.Relu, bias=qn_col[:])

@@ -1,7 +1,6 @@
 from contextlib import ExitStack
 
 import concourse.mybir as mybir
-from concourse.masks import make_identity
 
 F32 = mybir.dt.float32
 BF16 = mybir.dt.bfloat16
@@ -32,9 +31,9 @@ def tile_attend_student_topk_kernel(tc, qT, k_words, k_scales, kn, qn, offs, out
 
         offsets = sb.tile([P, N // 16], U16, name="offsets")
         scale_tab = sb.tile([P, T // 4], I32, name="scale_tab", align_bytes=64)
-        kn_tab = sb.tile([P, T], F32, name="kn_tab", tag="shared", align_bytes=64)
+        kn_tab = sb.tile([P, T], F32, name="kn_tab", align_bytes=64)
         word_tab = sb.tile([P, T], I32, name="word_tab", align_bytes=64)
-        q_raw = sb.tile([P, PACK, NQ], F32, name="q_raw", align_bytes=64)
+        q_raw = sb.tile([P, PACK, NQ], F32, name="q_raw", tag="k_codes", align_bytes=64)
         qn_col = sb.tile([P, 1], F32, name="qn_col")
         ident = sb.tile([P, P], F32, name="ident", align_bytes=64)
 
@@ -50,9 +49,11 @@ def tile_attend_student_topk_kernel(tc, qT, k_words, k_scales, kn, qn, offs, out
                 k_scales[0, 4 * quad : 4 * quad + 4, :].bitcast(I32),
             )
         nc.sync.dma_start(word_tab[:], k_words[0].rearrange("p n t -> p (n t)").bitcast(I32))
+        off_diagonal = sb.tile([P, P], I32, name="off_diagonal", tag="scalar_first", align_bytes=64)
+        nc.gpsimd.iota(off_diagonal[:], [[-1, P]], base=0, channel_multiplier=1)
         warm = sb.tile([P, 1], F32, name="warm")
-        nc.scalar.activation(warm[0:KN_ROW, :], kn_tab[0:KN_ROW, 0:1], ACT.Abs_reciprocal_sqrt, bias=1.0)
-        make_identity(nc, ident[:])
+        nc.scalar.activation(warm[:], off_diagonal[:, 0:1].bitcast(U32), ACT.Abs_reciprocal_sqrt, bias=1.0)
+        nc.scalar.activation(ident[:], off_diagonal[:].bitcast(U32), ACT.Relu, bias=1.0, scale=-1.0)
         nc.sync.dma_start(qn_col[:], qn[0])
 
         def half_offsets(h):
@@ -64,10 +65,10 @@ def tile_attend_student_topk_kernel(tc, qT, k_words, k_scales, kn, qn, offs, out
             nc.vector.tensor_copy(kn_row[:], kn_tab[:].indirect(half_offsets(h)))
             kn_rows.append(kn_row)
 
-        k_sc = sb.tile([P, N], U8, name="k_sc", tag="shared", align_bytes=64)
+        k_sc = sb.tile([P, N], U8, name="k_sc", align_bytes=64)
         nc.vector.tensor_copy(k_sc[:], scale_tab[:].bitcast(U8).indirect(offsets[:]))
 
-        q_bf = sb.tile([P, NQ, PACK], BF16, name="q_bf", align_bytes=64)
+        q_bf = sb.tile([P, NQ, PACK], BF16, name="q_bf", tag="scalar_first", align_bytes=64)
         nc.scalar.copy(q_bf[:], q_raw[:].rearrange("p j w -> p w j"))
         q_codes = sb.tile([P, NQ], U32, name="q_codes", align_bytes=64)
         q_sc = sb.tile([P, NQ], U8, name="q_sc", align_bytes=64)
@@ -99,15 +100,15 @@ def tile_attend_student_topk_kernel(tc, qT, k_words, k_scales, kn, qn, offs, out
             kn_alls.append(kn_all)
 
         dots = []
+        k_codes = sb.tile([P, N], U32, name="k_codes", tag="k_codes", align_bytes=64)
         for h in range(2):
-            k_codes = sb.tile([P, HALF], U32, name="k_codes%d" % h, align_bytes=64)
-            nc.vector.tensor_copy(k_codes[:], word_tab[:].bitcast(U32).indirect(half_offsets(h)))
+            nc.vector.tensor_copy(k_codes[:, h * HALF : (h + 1) * HALF], word_tab[:].bitcast(U32).indirect(half_offsets(h)))
             dot = ps.tile([P, HALF], F32, name="dot%d" % h)
             nc.tensor.matmul_mx(
                 out=dot[:],
                 lhsT=q_codes[:].bitcast(FP8X4),
                 lhsT_scale=q_sc[:],
-                rhs=k_codes[:].bitcast(FP8X4),
+                rhs=k_codes[:, h * HALF : (h + 1) * HALF].bitcast(FP8X4),
                 rhs_scale=k_sc[:, h * HALF : (h + 1) * HALF],
                 start=True,
                 stop=True,

@@ -42,12 +42,9 @@ def tile_attend_student_topk_kernel(tc, qT, k_words, k_scales, kn, qn, offs, out
 
         nc.sync.dma_start(offsets[:], offs)
         nc.sync.dma_start(kn_tab[KN_ROW:P, :], kn[0:1, :])
-        nc.sync.dma_start(q_raw[:], qT[0].rearrange("(p j) w -> p j w", j=PACK))
-        for quad in range(4):
-            nc.sync.dma_start(
-                scale_tab[32 * quad : 32 * quad + 4, :],
-                k_scales[0, 4 * quad : 4 * quad + 4, :].bitcast(I32),
-            )
+        nc.scalar.dma_start(q_raw[:], qT[0].rearrange("(p j) w -> p j w", j=PACK))
+        for row in range(4):
+            nc.sync.dma_start(scale_tab[row:P:32, :], k_scales[0, row:16:4, :].bitcast(I32))
         nc.sync.dma_start(word_tab[:], k_words[0].rearrange("p n t -> p (n t)").bitcast(I32))
         off_diagonal = sb.tile([P, P], I32, name="off_diagonal", tag="scalar_first", align_bytes=64)
         nc.gpsimd.iota(off_diagonal[:], [[-1, P]], base=0, channel_multiplier=1)

@@ -96,51 +96,61 @@ def tile_attend_student_topk_kernel(tc, qT, k_words, k_scales, kn, qn, offs, out
             nc.scalar.copy(kn_all[:], kn_spread[:])
             kn_alls.append(kn_all)
 
-        dots = []
         k_codes = sb.tile([P, N], U32, name="k_codes", tag="k_codes", align_bytes=64)
+        roots = [sb.tile([P, HALF], F32, name="root%d" % h, align_bytes=64) for h in range(2)]
+        dots = []
         for h in range(2):
-            nc.vector.tensor_copy(k_codes[:, h * HALF : (h + 1) * HALF], word_tab[:].bitcast(U32).indirect(half_offsets(h)))
-            dot = ps.tile([P, HALF], F32, name="dot%d" % h)
-            nc.tensor.matmul_mx(
-                out=dot[:],
-                lhsT=q_codes[:].bitcast(FP8X4),
-                lhsT_scale=q_sc[:],
-                rhs=k_codes[:, h * HALF : (h + 1) * HALF].bitcast(FP8X4),
-                rhs_scale=k_sc[:, h * HALF : (h + 1) * HALF],
-                start=True,
-                stop=True,
+            nc.vector.tensor_copy(
+                k_codes[:, h * HALF : (h + 1) * HALF], word_tab[:].bitcast(U32).indirect(half_offsets(h))
             )
-            dots.append(dot)
-
-        roots = []
-        sims = []
-        sums = []
-        for h in range(2):
-            part = sb.tile([P, HALF], F32, name="part%d" % h, align_bytes=64)
-            nc.vector.scalar_tensor_tensor(part[:], dots[h][:], -2.0, kn_alls[h][:], ALU.mult, ALU.add)
-            dist = sb.tile([P, HALF], F32, name="dist%d" % h, align_bytes=64)
-            if h == 0:
-                nc.scalar.activation(dist[:], part[:], ACT.Relu, bias=qn_col[:])
-            else:
-                nc.vector.tensor_scalar(dist[:], part[:], qn_col[:], 0.0, ALU.add, ALU.max)
-            root = sb.tile([P, HALF], F32, name="root%d" % h, align_bytes=64)
-            nc.scalar.activation(root[:], dist[:], ACT.Abs_reciprocal_sqrt, bias=1.0)
-            sim = sb.tile([P, HALF], F32, name="sim%d" % h, align_bytes=64)
-            total = sb.tile([P, 1], F32, name="total%d" % h)
-            if h == 0:
-                nc.vector.scalar_tensor_tensor(
-                    sim[:], root[:], 1.0, root[:], ALU.mult, ALU.mult, accum_out=total[:]
+            for j in range(2):
+                cols = slice(h * HALF + j * P, h * HALF + (j + 1) * P)
+                dot = ps.tile([P, P], F32, name="dot%d_%d" % (h, j))
+                nc.tensor.matmul_mx(
+                    out=dot[:],
+                    lhsT=q_codes[:].bitcast(FP8X4),
+                    lhsT_scale=q_sc[:],
+                    rhs=k_codes[:, cols].bitcast(FP8X4),
+                    rhs_scale=k_sc[:, cols],
+                    start=True,
+                    stop=True,
                 )
-            else:
-                nc.scalar.activation(sim[:], root[:], ACT.Square, accum_out=total[:])
-            roots.append(root)
-            sims.append(sim)
-            sums.append(total)
+                dots.append(dot)
+
+        for h in range(2):
+            parts = []
+            for j in range(2):
+                part = sb.tile([P, P], F32, name="part%d_%d" % (h, j), align_bytes=64)
+                nc.vector.scalar_tensor_tensor(
+                    part[:], dots[2 * h + j][:], -2.0, kn_alls[h][:, j * P : (j + 1) * P], ALU.mult, ALU.add
+                )
+                parts.append(part)
+            dists = []
+            for j in range(2):
+                dist = sb.tile([P, P], F32, name="dist%d_%d" % (h, j), align_bytes=64)
+                if h == 0:
+                    nc.scalar.activation(dist[:], parts[j][:], ACT.Relu, bias=qn_col[:])
+                else:
+                    nc.vector.tensor_scalar(dist[:], parts[j][:], qn_col[:], 0.0, ALU.add, ALU.max)
+                dists.append(dist)
+            for j in range(2):
+                nc.scalar.activation(
+                    roots[h][:, j * P : (j + 1) * P], dists[j][:], ACT.Abs_reciprocal_sqrt, bias=1.0
+                )
+
+        sim0 = sb.tile([P, HALF], F32, name="sim0", align_bytes=64)
+        total0 = sb.tile([P, 1], F32, name="total0")
+        nc.vector.scalar_tensor_tensor(
+            sim0[:], roots[0][:], 1.0, roots[0][:], ALU.mult, ALU.mult, accum_out=total0[:]
+        )
+        sim1 = sb.tile([P, HALF], F32, name="sim1", align_bytes=64)
+        total1 = sb.tile([P, 1], F32, name="total1")
+        nc.scalar.activation(sim1[:], roots[1][:], ACT.Square, accum_out=total1[:])
 
         norm = sb.tile([P, 1], F32, name="norm")
-        nc.scalar.activation(norm[:], sums[1][:], ACT.Abs_reciprocal_sqrt, bias=sums[0][:])
+        nc.scalar.activation(norm[:], total1[:], ACT.Abs_reciprocal_sqrt, bias=total0[:])
         res0 = sb.tile([P, HALF], F32, name="res0", align_bytes=64)
-        nc.vector.tensor_scalar(res0[:], sims[0][:], norm[:], norm[:], ALU.mult, ALU.mult)
+        nc.vector.tensor_scalar(res0[:], sim0[:], norm[:], norm[:], ALU.mult, ALU.mult)
         nc.sync.dma_start(out[0, :, 0:HALF], res0[:])
         res1 = sb.tile([P, HALF], F32, name="res1", align_bytes=64)
         nc.scalar.activation(res1[:], roots[1][:], ACT.Square, scale=norm[:])

@@ -1,6 +1,7 @@
 from contextlib import ExitStack
 
 import concourse.mybir as mybir
+from concourse.masks import make_identity
 
 F32 = mybir.dt.float32
 BF16 = mybir.dt.bfloat16
@@ -38,19 +39,18 @@ def tile_attend_student_topk_kernel(tc, qT, k_words, k_scales, kn, qn, offs, out
         ident = sb.tile([P, P], F32, name="ident", align_bytes=64)
 
         nc.vector.memset(scale_tab[:], 0)
+        nc.vector.memset(ident[:], 0.0)
         nc.vector.memset(kn_tab[0:KN_ROW, :], 0.0)
 
-        nc.sync.dma_start(offsets[:], offs)
         nc.sync.dma_start(kn_tab[KN_ROW:P, :], kn[0:1, :])
+        nc.sync.dma_start(offsets[:], offs)
         nc.scalar.dma_start(q_raw[:], qT[0].rearrange("(p j) w -> p j w", j=PACK))
         for row in range(4):
             nc.sync.dma_start(scale_tab[row:P:32, :], k_scales[0, row:16:4, :].bitcast(I32))
         nc.sync.dma_start(word_tab[:], k_words[0].rearrange("p n t -> p (n t)").bitcast(I32))
-        off_diagonal = sb.tile([P, P], I32, name="off_diagonal", tag="scalar_first", align_bytes=64)
-        nc.gpsimd.iota(off_diagonal[:], [[-1, P]], base=0, channel_multiplier=1)
-        warm = sb.tile([P, 1], F32, name="warm")
-        nc.scalar.activation(warm[:], off_diagonal[:, 0:1].bitcast(U32), ACT.Abs_reciprocal_sqrt, bias=1.0)
-        nc.scalar.activation(ident[:], off_diagonal[:].bitcast(U32), ACT.Relu, bias=1.0, scale=-1.0)
+        make_identity(nc, ident[:], nomemset=True)
+        warm = sb.tile([P, 1], F32, name="warm", tag="scalar_first", align_bytes=64)
+        nc.scalar.activation(warm[0:KN_ROW, :], kn_tab[0:KN_ROW, 0:1], ACT.Abs_reciprocal_sqrt, bias=1.0)
         nc.sync.dma_start(qn_col[:], qn[0])
 
         def half_offsets(h):

@@ -1,7 +1,6 @@
 from contextlib import ExitStack
 
 import concourse.mybir as mybir
-from concourse.masks import make_identity
 
 F32 = mybir.dt.float32
 BF16 = mybir.dt.bfloat16
@@ -36,10 +35,11 @@ def tile_attend_student_topk_kernel(tc, qT, k_words, k_scales, kn, qn, offs, out
         word_tab = sb.tile([P, T], I32, name="word_tab", align_bytes=64)
         q_raw = sb.tile([P, PACK, NQ], F32, name="q_raw", tag="k_codes", align_bytes=64)
         qn_col = sb.tile([P, 1], F32, name="qn_col")
+        zeros = sb.tile([P, P], F32, name="zeros", tag="zeros", align_bytes=64)
         ident = sb.tile([P, P], F32, name="ident", align_bytes=64)
 
         nc.vector.memset(scale_tab[:], 0)
-        nc.vector.memset(ident[:], 0.0)
+        nc.vector.memset(zeros[:], 0.0)
         nc.vector.memset(kn_tab[0:KN_ROW, :], 0.0)
 
         nc.sync.dma_start(kn_tab[KN_ROW:P, :], kn[0:1, :])
@@ -48,9 +48,19 @@ def tile_attend_student_topk_kernel(tc, qT, k_words, k_scales, kn, qn, offs, out
         for row in range(4):
             nc.sync.dma_start(scale_tab[row:P:32, :], k_scales[0, row:16:4, :].bitcast(I32))
         nc.sync.dma_start(word_tab[:], k_words[0].rearrange("p n t -> p (n t)").bitcast(I32))
-        make_identity(nc, ident[:], nomemset=True)
-        warm = sb.tile([P, 1], F32, name="warm", tag="scalar_first", align_bytes=64)
-        nc.scalar.activation(warm[0:KN_ROW, :], kn_tab[0:KN_ROW, 0:1], ACT.Abs_reciprocal_sqrt, bias=1.0)
+        nc.gpsimd.affine_select(
+            out=ident[:],
+            in_=zeros[:],
+            compare_op=ALU.not_equal,
+            fill=1.0,
+            base=0,
+            pattern=[[-1, P]],
+            channel_multiplier=1,
+        )
+        warm = sb.tile([P, 1], F32, name="warm")
+        nc.scalar.activation(
+            warm[0:KN_ROW, :], kn_tab[0:KN_ROW, 0:1], ACT.Abs_reciprocal_sqrt, bias=1.0, scale=zeros[0:KN_ROW, 0:1]
+        )
         nc.sync.dma_start(qn_col[:], qn[0])
 
         def half_offsets(h):
@@ -65,7 +75,7 @@ def tile_attend_student_topk_kernel(tc, qT, k_words, k_scales, kn, qn, offs, out
         k_sc = sb.tile([P, N], U8, name="k_sc", align_bytes=64)
         nc.vector.tensor_copy(k_sc[:], scale_tab[:].bitcast(U8).indirect(offsets[:]))
 
-        q_bf = sb.tile([P, NQ, PACK], BF16, name="q_bf", tag="scalar_first", align_bytes=64)
+        q_bf = sb.tile([P, NQ, PACK], BF16, name="q_bf", tag="zeros", align_bytes=64)
         nc.scalar.copy(q_bf[:], q_raw[:].rearrange("p j w -> p w j"))
         q_codes = sb.tile([P, NQ], U32, name="q_codes", align_bytes=64)
         q_sc = sb.tile([P, NQ], U8, name="q_sc", align_bytes=64)

@@ -35,7 +35,7 @@ def tile_attend_student_topk_kernel(tc, qT, k_words, k_scales, kn, qn, offs, out
         word_tab = sb.tile([P, T], I32, name="word_tab", align_bytes=64)
         q_raw = sb.tile([P, PACK, NQ], F32, name="q_raw", tag="k_codes", align_bytes=64)
         qn_col = sb.tile([P, 1], F32, name="qn_col")
-        zeros = sb.tile([P, P], F32, name="zeros", tag="zeros", align_bytes=64)
+        zeros = sb.tile([P, P], F32, name="zeros", align_bytes=64)
         ident = sb.tile([P, P], F32, name="ident", align_bytes=64)
 
         nc.vector.memset(scale_tab[:], 0)
@@ -58,9 +58,7 @@ def tile_attend_student_topk_kernel(tc, qT, k_words, k_scales, kn, qn, offs, out
             channel_multiplier=1,
         )
         warm = sb.tile([P, 1], F32, name="warm")
-        nc.scalar.activation(
-            warm[0:KN_ROW, :], kn_tab[0:KN_ROW, 0:1], ACT.Abs_reciprocal_sqrt, bias=1.0, scale=zeros[0:KN_ROW, 0:1]
-        )
+        nc.scalar.activation(warm[:], zeros[:, 0:1], ACT.Abs_reciprocal_sqrt, bias=1.0)
         nc.sync.dma_start(qn_col[:], qn[0])
 
         def half_offsets(h):
@@ -69,14 +67,14 @@ def tile_attend_student_topk_kernel(tc, qT, k_words, k_scales, kn, qn, offs, out
         kn_rows = []
         for h in range(2):
             kn_row = sb.tile([P, HALF], F32, name="kn_row%d" % h, align_bytes=64)
-            nc.vector.tensor_copy(kn_row[:], kn_tab[:].indirect(half_offsets(h)))
+            nc.scalar.activation(kn_row[:], kn_tab[:].indirect(half_offsets(h)), ACT.Copy)
             kn_rows.append(kn_row)
 
         k_sc = sb.tile([P, N], U8, name="k_sc", align_bytes=64)
         nc.vector.tensor_copy(k_sc[:], scale_tab[:].bitcast(U8).indirect(offsets[:]))
 
-        q_bf = sb.tile([P, NQ, PACK], BF16, name="q_bf", tag="zeros", align_bytes=64)
-        nc.scalar.copy(q_bf[:], q_raw[:].rearrange("p j w -> p w j"))
+        q_bf = sb.tile([P, NQ, PACK], BF16, name="q_bf", align_bytes=64)
+        nc.vector.tensor_copy(q_bf[:], q_raw[:].rearrange("p j w -> p w j"))
         q_codes = sb.tile([P, NQ], U32, name="q_codes", align_bytes=64)
         q_sc = sb.tile([P, NQ], U8, name="q_sc", align_bytes=64)
         nc.vector.quantize_mx(

@@ -105,14 +105,17 @@ def tile_attend_student_topk_kernel(tc, qT, k_words, k_scales, kn, qn, offs, out
             kn_alls.append(kn_all)
 
         k_codes = sb.tile([P, N], U32, name="k_codes", tag="k_codes", align_bytes=64)
-        roots = [sb.tile([P, HALF], F32, name="root%d" % h, align_bytes=64) for h in range(2)]
         dots = []
         for h in range(2):
-            nc.vector.tensor_copy(
-                k_codes[:, h * HALF : (h + 1) * HALF], word_tab[:].bitcast(U32).indirect(half_offsets(h))
-            )
+            if h == 0:
+                nc.vector.tensor_copy(k_codes[:, 0:HALF], word_tab[:].bitcast(U32).indirect(half_offsets(0)))
             for j in range(2):
                 cols = slice(h * HALF + j * P, h * HALF + (j + 1) * P)
+                if h == 1:
+                    nc.vector.tensor_copy(
+                        k_codes[:, cols],
+                        word_tab[:].bitcast(U32).indirect(offsets[:, cols.start // 16 : cols.stop // 16]),
+                    )
                 dot = ps.tile([P, P], F32, name="dot%d_%d" % (h, j))
                 nc.tensor.matmul_mx(
                     out=dot[:],
@@ -125,41 +128,51 @@ def tile_attend_student_topk_kernel(tc, qT, k_words, k_scales, kn, qn, offs, out
                 )
                 dots.append(dot)
 
-        for h in range(2):
-            parts = []
-            for j in range(2):
-                part = sb.tile([P, P], F32, name="part%d_%d" % (h, j), align_bytes=64)
-                nc.vector.scalar_tensor_tensor(
-                    part[:], dots[2 * h + j][:], -2.0, kn_alls[h][:, j * P : (j + 1) * P], ALU.mult, ALU.add
-                )
-                parts.append(part)
-            dists = []
-            for j in range(2):
-                dist = sb.tile([P, P], F32, name="dist%d_%d" % (h, j), align_bytes=64)
-                if h == 0:
-                    nc.scalar.activation(dist[:], parts[j][:], ACT.Relu, bias=qn_col[:])
-                else:
-                    nc.vector.tensor_scalar(dist[:], parts[j][:], qn_col[:], 0.0, ALU.add, ALU.max)
-                dists.append(dist)
-            for j in range(2):
-                nc.scalar.activation(
-                    roots[h][:, j * P : (j + 1) * P], dists[j][:], ACT.Abs_reciprocal_sqrt, bias=1.0
-                )
+        root = sb.tile([P, N], F32, name="root", align_bytes=64)
+        parts = [sb.tile([P, P], F32, name="part%d" % i, align_bytes=64) for i in range(4)]
+        dists = [sb.tile([P, P], F32, name="dist%d" % i, align_bytes=64) for i in range(4)]
 
-        sim0 = sb.tile([P, HALF], F32, name="sim0", align_bytes=64)
+        def add_kn(i):
+            kn_piece = kn_alls[i // 2][:, i % 2 * P : (i % 2 + 1) * P]
+            nc.vector.scalar_tensor_tensor(parts[i][:], dots[i][:], -2.0, kn_piece, ALU.mult, ALU.add)
+
+        def clamp_scalar(i):
+            nc.scalar.activation(dists[i][:], parts[i][:], ACT.Relu, bias=qn_col[:])
+
+        def clamp_vector(i):
+            nc.vector.tensor_scalar(dists[i][:], parts[i][:], qn_col[:], 0.0, ALU.add, ALU.max)
+
+        def inv_root(i):
+            nc.scalar.activation(root[:, i * P : (i + 1) * P], dists[i][:], ACT.Abs_reciprocal_sqrt, bias=1.0)
+
+        add_kn(0)
+        add_kn(1)
+        clamp_scalar(0)
+        clamp_scalar(1)
+        inv_root(0)
+        inv_root(1)
+        add_kn(2)
+        clamp_vector(2)
+        inv_root(2)
+        add_kn(3)
+        clamp_vector(3)
+        inv_root(3)
+
+        CUT = 2 * P
+        sim0 = sb.tile([P, CUT], F32, name="sim0", align_bytes=64)
         total0 = sb.tile([P, 1], F32, name="total0")
         nc.vector.scalar_tensor_tensor(
-            sim0[:], roots[0][:], 1.0, roots[0][:], ALU.mult, ALU.mult, accum_out=total0[:]
+            sim0[:], root[:, 0:CUT], 1.0, root[:, 0:CUT], ALU.mult, ALU.mult, accum_out=total0[:]
         )
-        sim1 = sb.tile([P, HALF], F32, name="sim1", align_bytes=64)
+        sim1 = sb.tile([P, N - CUT], F32, name="sim1", align_bytes=64)
         total1 = sb.tile([P, 1], F32, name="total1")
-        nc.scalar.activation(sim1[:], roots[1][:], ACT.Square, accum_out=total1[:])
+        nc.scalar.activation(sim1[:], root[:, CUT:N], ACT.Square, accum_out=total1[:])
 
         norm = sb.tile([P, 1], F32, name="norm")
         nc.scalar.activation(norm[:], total1[:], ACT.Abs_reciprocal_sqrt, bias=total0[:])
-        res0 = sb.tile([P, HALF], F32, name="res0", align_bytes=64)
+        res0 = sb.tile([P, CUT], F32, name="res0", align_bytes=64)
         nc.vector.tensor_scalar(res0[:], sim0[:], norm[:], norm[:], ALU.mult, ALU.mult)
-        nc.sync.dma_start(out[0, :, 0:HALF], res0[:])
-        res1 = sb.tile([P, HALF], F32, name="res1", align_bytes=64)
-        nc.scalar.activation(res1[:], roots[1][:], ACT.Square, scale=norm[:])
-        nc.scalar.dma_start(out[0, :, HALF:N], res1[:])
+        nc.sync.dma_start(out[0, :, 0:CUT], res0[:])
+        res1 = sb.tile([P, N - CUT], F32, name="res1", align_bytes=64)
+        nc.scalar.activation(res1[:], root[:, CUT:N], ACT.Square, scale=norm[:])
+        nc.scalar.dma_start(out[0, :, CUT:N], res1[:])

@@ -107,15 +107,12 @@ def tile_attend_student_topk_kernel(tc, qT, k_words, k_scales, kn, qn, offs, out
         k_codes = sb.tile([P, N], U32, name="k_codes", tag="k_codes", align_bytes=64)
         dots = []
         for h in range(2):
-            if h == 0:
-                nc.vector.tensor_copy(k_codes[:, 0:HALF], word_tab[:].bitcast(U32).indirect(half_offsets(0)))
             for j in range(2):
                 cols = slice(h * HALF + j * P, h * HALF + (j + 1) * P)
-                if h == 1:
-                    nc.vector.tensor_copy(
-                        k_codes[:, cols],
-                        word_tab[:].bitcast(U32).indirect(offsets[:, cols.start // 16 : cols.stop // 16]),
-                    )
+                nc.vector.tensor_copy(
+                    k_codes[:, cols],
+                    word_tab[:].bitcast(U32).indirect(offsets[:, cols.start // 16 : cols.stop // 16]),
+                )
                 dot = ps.tile([P, P], F32, name="dot%d_%d" % (h, j))
                 nc.tensor.matmul_mx(
                     out=dot[:],
@@ -132,18 +129,20 @@ def tile_attend_student_topk_kernel(tc, qT, k_words, k_scales, kn, qn, offs, out
         parts = [sb.tile([P, P], F32, name="part%d" % i, align_bytes=64) for i in range(4)]
         dists = [sb.tile([P, P], F32, name="dist%d" % i, align_bytes=64) for i in range(4)]
 
-        def add_kn(i):
-            kn_piece = kn_alls[i // 2][:, i % 2 * P : (i % 2 + 1) * P]
-            nc.vector.scalar_tensor_tensor(parts[i][:], dots[i][:], -2.0, kn_piece, ALU.mult, ALU.add)
+        def add_kn(i, lo=0, hi=P):
+            kn_piece = kn_alls[i // 2][:, i % 2 * P + lo : i % 2 * P + hi]
+            nc.vector.scalar_tensor_tensor(parts[i][:, lo:hi], dots[i][:, lo:hi], -2.0, kn_piece, ALU.mult, ALU.add)
 
         def clamp_scalar(i):
             nc.scalar.activation(dists[i][:], parts[i][:], ACT.Relu, bias=qn_col[:])
 
-        def clamp_vector(i):
-            nc.vector.tensor_scalar(dists[i][:], parts[i][:], qn_col[:], 0.0, ALU.add, ALU.max)
+        def clamp_vector(i, lo=0, hi=P):
+            nc.vector.tensor_scalar(dists[i][:, lo:hi], parts[i][:, lo:hi], qn_col[:], 0.0, ALU.add, ALU.max)
 
-        def inv_root(i):
-            nc.scalar.activation(root[:, i * P : (i + 1) * P], dists[i][:], ACT.Abs_reciprocal_sqrt, bias=1.0)
+        def inv_root(i, lo=0, hi=P):
+            nc.scalar.activation(
+                root[:, i * P + lo : i * P + hi], dists[i][:, lo:hi], ACT.Abs_reciprocal_sqrt, bias=1.0
+            )
 
         add_kn(0)
         add_kn(1)
@@ -152,11 +151,14 @@ def tile_attend_student_topk_kernel(tc, qT, k_words, k_scales, kn, qn, offs, out
         inv_root(0)
         inv_root(1)
         add_kn(2)
+        add_kn(3, 0, P // 2)
+        add_kn(3, P // 2, P)
         clamp_vector(2)
         inv_root(2)
-        add_kn(3)
-        clamp_vector(3)
-        inv_root(3)
+        clamp_vector(3, 0, P // 2)
+        clamp_vector(3, P // 2, P)
+        inv_root(3, 0, P // 2)
+        inv_root(3, P // 2, P)
 
         CUT = 2 * P
         sim0 = sb.tile([P, CUT], F32, name="sim0", align_bytes=64)

@@ -30,7 +30,7 @@ def tile_attend_student_topk_kernel(tc, qT, k_words, k_scales, kn, qn, offs, out
         ps = ctx.enter_context(tc.psum_pool(name="ps", bufs=1))
 
         offsets = sb.tile([P, N // 16], U16, name="offsets")
-        scale_tab = sb.tile([P, T // 4], I32, name="scale_tab", align_bytes=64)
+        scale_tab = sb.tile([P, T // 4], I32, name="scale_tab", tag="scale_tab", align_bytes=64)
         kn_tab = sb.tile([P, T], F32, name="kn_tab", align_bytes=64)
         word_tab = sb.tile([P, T], I32, name="word_tab", align_bytes=64)
         q_raw = sb.tile([P, PACK, NQ], F32, name="q_raw", tag="k_codes", align_bytes=64)
@@ -38,15 +38,17 @@ def tile_attend_student_topk_kernel(tc, qT, k_words, k_scales, kn, qn, offs, out
         zeros = sb.tile([P, P], F32, name="zeros", align_bytes=64)
         ident = sb.tile([P, P], F32, name="ident", align_bytes=64)
 
+        k_sc = sb.tile([P, N // 4], I32, name="k_sc", align_bytes=64)
+
         nc.vector.memset(scale_tab[:], 0)
         nc.vector.memset(zeros[:], 0.0)
+        nc.vector.memset(k_sc[:], 0)
         nc.vector.memset(kn_tab[0:KN_ROW, :], 0.0)
 
         nc.sync.dma_start(kn_tab[KN_ROW:P, :], kn[0:1, :])
         nc.sync.dma_start(offsets[:], offs)
         nc.scalar.dma_start(q_raw[:], qT[0].rearrange("(p j) w -> p j w", j=PACK))
-        for row in range(4):
-            nc.sync.dma_start(scale_tab[row:P:32, :], k_scales[0, row:16:4, :].bitcast(I32))
+        nc.sync.dma_start(scale_tab[32:96:4, :], k_scales[0].bitcast(I32))
         nc.sync.dma_start(word_tab[:], k_words[0].rearrange("p n t -> p (n t)").bitcast(I32))
         nc.gpsimd.affine_select(
             out=ident[:],
@@ -70,18 +72,24 @@ def tile_attend_student_topk_kernel(tc, qT, k_words, k_scales, kn, qn, offs, out
             nc.scalar.activation(kn_row[:], kn_tab[:].indirect(half_offsets(h)), ACT.Copy)
             kn_rows.append(kn_row)
 
-        k_sc = sb.tile([P, N], U8, name="k_sc", align_bytes=64)
-        nc.vector.tensor_copy(k_sc[:], scale_tab[:].bitcast(U8).indirect(offsets[:]))
+        sc_picked = sb.tile([P, N], U8, name="sc_picked", align_bytes=64)
+        nc.vector.tensor_copy(sc_picked[:], scale_tab[:].bitcast(U8).indirect(offsets[:]))
+        for row in range(4):
+            queue = nc.sync if row % 2 == 0 else nc.scalar
+            queue.dma_start(k_sc[row:P:32, :], sc_picked[32 + 4 * row : 96 : 16, :].bitcast(I32))
 
-        q_bf = sb.tile([P, NQ, PACK], BF16, name="q_bf", align_bytes=64)
-        nc.vector.tensor_copy(q_bf[:], q_raw[:].rearrange("p j w -> p w j"))
+        q_bf = sb.tile([P, NQ, PACK], BF16, name="q_bf", tag="scale_tab", align_bytes=64)
+        q_halves = [slice(h * NQ // 2, (h + 1) * NQ // 2) for h in range(2)]
+        for rows in q_halves:
+            nc.vector.tensor_copy(q_bf[:, rows, :], q_raw[:, :, rows].rearrange("p j w -> p w j"))
         q_codes = sb.tile([P, NQ], U32, name="q_codes", align_bytes=64)
         q_sc = sb.tile([P, NQ], U8, name="q_sc", align_bytes=64)
-        nc.vector.quantize_mx(
-            out=q_codes[:].bitcast(FP8X4),
-            scales=q_sc[:],
-            in_=q_bf[:].rearrange("p w j -> p (w j)"),
-        )
+        for rows in q_halves:
+            nc.vector.quantize_mx(
+                out=q_codes[:, rows].bitcast(FP8X4),
+                scales=q_sc[:, rows],
+                in_=q_bf[:, rows, :].rearrange("p w j -> p (w j)"),
+            )
 
         kn_colss = []
         for h in range(2):
@@ -119,7 +127,7 @@ def tile_attend_student_topk_kernel(tc, qT, k_words, k_scales, kn, qn, offs, out
                     lhsT=q_codes[:].bitcast(FP8X4),
                     lhsT_scale=q_sc[:],
                     rhs=k_codes[:, cols].bitcast(FP8X4),
-                    rhs_scale=k_sc[:, cols],
+                    rhs_scale=k_sc[:].bitcast(U8)[:, cols],
                     start=True,
                     stop=True,
                 )

@@ -63,20 +63,19 @@ def tile_attend_student_topk_kernel(tc, qT, k_words, k_scales, kn, qn, offs, out
         nc.scalar.activation(warm[:], zeros[:, 0:1], ACT.Abs_reciprocal_sqrt, bias=1.0)
         nc.sync.dma_start(qn_col[:], qn[0])
 
-        def half_offsets(h):
-            return offsets[:, h * HALF // 16 : (h + 1) * HALF // 16]
+        def piece_offsets(i):
+            return offsets[:, i * P // 16 : (i + 1) * P // 16]
 
         kn_rows = []
-        for h in range(2):
-            kn_row = sb.tile([P, HALF], F32, name="kn_row%d" % h, align_bytes=64)
-            nc.scalar.activation(kn_row[:], kn_tab[:].indirect(half_offsets(h)), ACT.Copy)
+        for i in range(4):
+            kn_row = sb.tile([P, P], F32, name="kn_row%d" % i, align_bytes=64)
+            nc.scalar.activation(kn_row[:], kn_tab[:].indirect(piece_offsets(i)), ACT.Copy)
             kn_rows.append(kn_row)
 
         sc_picked = sb.tile([P, N], U8, name="sc_picked", align_bytes=64)
         nc.vector.tensor_copy(sc_picked[:], scale_tab[:].bitcast(U8).indirect(offsets[:]))
         for row in range(4):
-            queue = nc.sync if row % 2 == 0 else nc.scalar
-            queue.dma_start(k_sc[row:P:32, :], sc_picked[32 + 4 * row : 96 : 16, :].bitcast(I32))
+            nc.sync.dma_start(k_sc[row:P:32, :], sc_picked[32 + 4 * row : 96 : 16, :].bitcast(I32))
 
         q_bf = sb.tile([P, NQ, PACK], BF16, name="q_bf", tag="scale_tab", align_bytes=64)
         q_halves = [slice(h * NQ // 2, (h + 1) * NQ // 2) for h in range(2)]
@@ -91,24 +90,18 @@ def tile_attend_student_topk_kernel(tc, qT, k_words, k_scales, kn, qn, offs, out
                 in_=q_bf[:, rows, :].rearrange("p w j -> p (w j)"),
             )
 
-        kn_colss = []
-        for h in range(2):
-            kn_turned = ps.tile([P, 2, P], F32, name="kn_turned%d" % h)
-            for j in range(2):
-                nc.tensor.transpose(kn_turned[:, j, :], kn_rows[h][:, j * P : (j + 1) * P], ident[:])
-            kn_cols = sb.tile([P, 2], F32, name="kn_cols%d" % h)
-            nc.scalar.copy(kn_cols[:], kn_turned[:, :, KN_ROW])
-            kn_colss.append(kn_cols)
+        kn_cols = []
+        for i in range(4):
+            kn_turned = ps.tile([P, P], F32, name="kn_turned%d" % i, tag="bank%d" % i)
+            nc.tensor.transpose(kn_turned[:], kn_rows[i][:], ident[:])
+            kn_col = sb.tile([P, 1], F32, name="kn_col%d" % i)
+            nc.scalar.copy(kn_col[:], kn_turned[:, KN_ROW : KN_ROW + 1])
+            kn_cols.append(kn_col)
         kn_alls = []
-        for h in range(2):
-            kn_spread = ps.tile([P, HALF], F32, name="kn_spread%d" % h)
-            for j in range(2):
-                nc.tensor.transpose(
-                    kn_spread[:, j * P : (j + 1) * P],
-                    kn_colss[h][:, j : j + 1].to_broadcast([P, P]),
-                    ident[:],
-                )
-            kn_all = sb.tile([P, HALF], F32, name="kn_all%d" % h, align_bytes=64)
+        for i in range(4):
+            kn_spread = ps.tile([P, P], F32, name="kn_spread%d" % i)
+            nc.tensor.transpose(kn_spread[:], kn_cols[i][:].to_broadcast([P, P]), ident[:])
+            kn_all = sb.tile([P, P], F32, name="kn_all%d" % i, align_bytes=64)
             nc.scalar.copy(kn_all[:], kn_spread[:])
             kn_alls.append(kn_all)
 
@@ -121,7 +114,7 @@ def tile_attend_student_topk_kernel(tc, qT, k_words, k_scales, kn, qn, offs, out
                     k_codes[:, cols],
                     word_tab[:].bitcast(U32).indirect(offsets[:, cols.start // 16 : cols.stop // 16]),
                 )
-                dot = ps.tile([P, P], F32, name="dot%d_%d" % (h, j))
+                dot = ps.tile([P, P], F32, name="dot%d_%d" % (h, j), tag="bank%d" % (2 * h + j))
                 nc.tensor.matmul_mx(
                     out=dot[:],
                     lhsT=q_codes[:].bitcast(FP8X4),
@@ -138,7 +131,7 @@ def tile_attend_student_topk_kernel(tc, qT, k_words, k_scales, kn, qn, offs, out
         dists = [sb.tile([P, P], F32, name="dist%d" % i, align_bytes=64) for i in range(4)]
 
         def add_kn(i, lo=0, hi=P):
-            kn_piece = kn_alls[i // 2][:, i % 2 * P + lo : i % 2 * P + hi]
+            kn_piece = kn_alls[i][:, lo:hi]
             nc.vector.scalar_tensor_tensor(parts[i][:, lo:hi], dots[i][:, lo:hi], -2.0, kn_piece, ALU.mult, ALU.add)
 
         def clamp_scalar(i):

@@ -48,7 +48,7 @@ def tile_attend_student_topk_kernel(tc, qT, k_words, k_scales, kn, qn, offs, out
         nc.sync.dma_start(kn_tab[KN_ROW:P, :], kn[0:1, :])
         nc.sync.dma_start(offsets[:], offs)
         nc.scalar.dma_start(q_raw[:], qT[0].rearrange("(p j) w -> p j w", j=PACK))
-        nc.sync.dma_start(scale_tab[32:96:4, :], k_scales[0].bitcast(I32))
+        nc.sync.dma_start(scale_tab[0:16, :], k_scales[0].bitcast(I32))
         nc.sync.dma_start(word_tab[:], k_words[0].rearrange("p n t -> p (n t)").bitcast(I32))
         nc.gpsimd.affine_select(
             out=ident[:],
@@ -73,9 +73,17 @@ def tile_attend_student_topk_kernel(tc, qT, k_words, k_scales, kn, qn, offs, out
             kn_rows.append(kn_row)
 
         sc_picked = sb.tile([P, N], U8, name="sc_picked", align_bytes=64)
-        nc.vector.tensor_copy(sc_picked[:], scale_tab[:].bitcast(U8).indirect(offsets[:]))
-        for row in range(4):
-            nc.sync.dma_start(k_sc[row:P:32, :], sc_picked[32 + 4 * row : 96 : 16, :].bitcast(I32))
+        for h in range(2):
+            cols = slice(h * HALF, (h + 1) * HALF)
+            nc.vector.tensor_copy(
+                sc_picked[:, cols],
+                scale_tab[:].bitcast(U8).indirect(offsets[:, cols.start // 16 : cols.stop // 16]),
+            )
+            for quad in range(1, 4):
+                nc.sync.dma_start(
+                    k_sc[32 * quad : 32 * quad + 4, cols.start // 4 : cols.stop // 4],
+                    sc_picked[4 * quad : 4 * quad + 4, cols].bitcast(I32),
+                )
 
         q_bf = sb.tile([P, NQ, PACK], BF16, name="q_bf", tag="scale_tab", align_bytes=64)
         q_halves = [slice(h * NQ // 2, (h + 1) * NQ // 2) for h in range(2)]
@@ -89,6 +97,8 @@ def tile_attend_student_topk_kernel(tc, qT, k_words, k_scales, kn, qn, offs, out
                 scales=q_sc[:, rows],
                 in_=q_bf[:, rows, :].rearrange("p w j -> p (w j)"),
             )
+
+        nc.vector.tensor_copy(k_sc[0:4, :], sc_picked[0:4, :].bitcast(I32))
 
         kn_cols = []
         for i in range(4):
@@ -127,7 +137,7 @@ def tile_attend_student_topk_kernel(tc, qT, k_words, k_scales, kn, qn, offs, out
                 dots.append(dot)
 
         root = sb.tile([P, N], F32, name="root", align_bytes=64)
-        parts = [sb.tile([P, P], F32, name="part%d" % i, align_bytes=64) for i in range(4)]
+        parts = [sb.tile([P, P], F32, name="part%d" % i, tag="part%d" % i, align_bytes=64) for i in range(4)]
         dists = [sb.tile([P, P], F32, name="dist%d" % i, align_bytes=64) for i in range(4)]
 
         def add_kn(i, lo=0, hi=P):
@@ -162,7 +172,7 @@ def tile_attend_student_topk_kernel(tc, qT, k_words, k_scales, kn, qn, offs, out
         inv_root(3, P // 2, P)
 
         CUT = 2 * P
-        sim0 = sb.tile([P, CUT], F32, name="sim0", align_bytes=64)
+        sim0 = sb.tile([P, CUT], F32, name="sim0", tag="part3", align_bytes=64)
         total0 = sb.tile([P, 1], F32, name="total0")
         nc.vector.scalar_tensor_tensor(
             sim0[:], root[:, 0:CUT], 1.0, root[:, 0:CUT], ALU.mult, ALU.mult, accum_out=total0[:]

@@ -42,7 +42,6 @@ def tile_attend_student_topk_kernel(tc, qT, k_words, k_scales, kn, qn, offs, out
 
         nc.vector.memset(scale_tab[:], 0)
         nc.vector.memset(zeros[:], 0.0)
-        nc.vector.memset(k_sc[:], 0)
         nc.vector.memset(kn_tab[0:KN_ROW, :], 0.0)
 
         nc.sync.dma_start(kn_tab[KN_ROW:P, :], kn[0:1, :])
@@ -89,6 +88,7 @@ def tile_attend_student_topk_kernel(tc, qT, k_words, k_scales, kn, qn, offs, out
         q_halves = [slice(h * NQ // 2, (h + 1) * NQ // 2) for h in range(2)]
         for rows in q_halves:
             nc.vector.tensor_copy(q_bf[:, rows, :], q_raw[:, :, rows].rearrange("p j w -> p w j"))
+        nc.vector.tensor_copy(k_sc[0:4, :], sc_picked[0:4, :].bitcast(I32))
         q_codes = sb.tile([P, NQ], U32, name="q_codes", align_bytes=64)
         q_sc = sb.tile([P, NQ], U8, name="q_sc", align_bytes=64)
         for rows in q_halves:
@@ -97,8 +97,6 @@ def tile_attend_student_topk_kernel(tc, qT, k_words, k_scales, kn, qn, offs, out
                 scales=q_sc[:, rows],
                 in_=q_bf[:, rows, :].rearrange("p w j -> p (w j)"),
             )
-
-        nc.vector.tensor_copy(k_sc[0:4, :], sc_picked[0:4, :].bitcast(I32))
 
         kn_cols = []
         for i in range(4):

@@ -44,8 +44,8 @@ def tile_attend_student_topk_kernel(tc, qT, k_words, k_scales, kn, qn, offs, out
         nc.vector.memset(zeros[:], 0.0)
         nc.vector.memset(kn_tab[0:KN_ROW, :], 0.0)
 
-        nc.sync.dma_start(kn_tab[KN_ROW:P, :], kn[0:1, :])
         nc.sync.dma_start(offsets[:], offs)
+        nc.sync.dma_start(kn_tab[KN_ROW:P, :], kn[0:1, :])
         nc.scalar.dma_start(q_raw[:], qT[0].rearrange("(p j) w -> p j w", j=PACK))
         nc.sync.dma_start(scale_tab[0:16, :], k_scales[0].bitcast(I32))
         nc.sync.dma_start(word_tab[:], k_words[0].rearrange("p n t -> p (n t)").bitcast(I32))

from contextlib import ExitStack

import concourse.mybir as mybir

F32 = mybir.dt.float32
BF16 = mybir.dt.bfloat16
I32 = mybir.dt.int32
U32 = mybir.dt.uint32
U16 = mybir.dt.uint16
U8 = mybir.dt.uint8
FP8X4 = mybir.dt.float8_e4m3fn_x4
ACT = mybir.ActivationFunctionType
ALU = mybir.AluOpType

P = 128
PACK = 4
T = 2048
N = 512
NQ = 128
HALF = N // 2
KN_ROW = P - 1

FLOPS = 2 * NQ * N * P * PACK


def tile_attend_student_topk_kernel(tc, qT, k_words, k_scales, kn, qn, offs, out):
    nc = tc.nc
    with ExitStack() as ctx:
        sb = ctx.enter_context(tc.tile_pool(name="sb", bufs=1))
        ps = ctx.enter_context(tc.psum_pool(name="ps", bufs=1))

        offsets = sb.tile([P, N // 16], U16, name="offsets")
        scale_tab = sb.tile([P, T // 4], I32, name="scale_tab", tag="scale_tab", align_bytes=64)
        kn_tab = sb.tile([P, T], F32, name="kn_tab", align_bytes=64)
        word_tab = sb.tile([P, T], I32, name="word_tab", align_bytes=64)
        q_raw = sb.tile([P, PACK, NQ], F32, name="q_raw", tag="k_codes", align_bytes=64)
        qn_col = sb.tile([P, 1], F32, name="qn_col")
        zeros = sb.tile([P, P], F32, name="zeros", align_bytes=64)
        ident = sb.tile([P, P], F32, name="ident", align_bytes=64)

        k_sc = sb.tile([P, N // 4], I32, name="k_sc", align_bytes=64)

        nc.vector.memset(scale_tab[:], 0)
        nc.vector.memset(zeros[:], 0.0)
        nc.vector.memset(kn_tab[0:KN_ROW, :], 0.0)

        nc.sync.dma_start(offsets[:], offs)
        nc.sync.dma_start(kn_tab[KN_ROW:P, :], kn[0:1, :])
        nc.scalar.dma_start(q_raw[:], qT[0].rearrange("(p j) w -> p j w", j=PACK))
        nc.sync.dma_start(scale_tab[0:16, :], k_scales[0].bitcast(I32))
        nc.sync.dma_start(word_tab[:], k_words[0].rearrange("p n t -> p (n t)").bitcast(I32))
        nc.gpsimd.affine_select(
            out=ident[:],
            in_=zeros[:],
            compare_op=ALU.not_equal,
            fill=1.0,
            base=0,
            pattern=[[-1, P]],
            channel_multiplier=1,
        )
        warm = sb.tile([P, 1], F32, name="warm")
        nc.scalar.activation(warm[:], zeros[:, 0:1], ACT.Abs_reciprocal_sqrt, bias=1.0)
        nc.sync.dma_start(qn_col[:], qn[0])

        def piece_offsets(i):
            return offsets[:, i * P // 16 : (i + 1) * P // 16]

        kn_rows = []
        for i in range(4):
            kn_row = sb.tile([P, P], F32, name="kn_row%d" % i, align_bytes=64)
            nc.scalar.activation(kn_row[:], kn_tab[:].indirect(piece_offsets(i)), ACT.Copy)
            kn_rows.append(kn_row)

        sc_picked = sb.tile([P, N], U8, name="sc_picked", align_bytes=64)
        for h in range(2):
            cols = slice(h * HALF, (h + 1) * HALF)
            nc.vector.tensor_copy(
                sc_picked[:, cols],
                scale_tab[:].bitcast(U8).indirect(offsets[:, cols.start // 16 : cols.stop // 16]),
            )
            for quad in range(1, 4):
                nc.sync.dma_start(
                    k_sc[32 * quad : 32 * quad + 4, cols.start // 4 : cols.stop // 4],
                    sc_picked[4 * quad : 4 * quad + 4, cols].bitcast(I32),
                )

        q_bf = sb.tile([P, NQ, PACK], BF16, name="q_bf", tag="scale_tab", align_bytes=64)
        q_halves = [slice(h * NQ // 2, (h + 1) * NQ // 2) for h in range(2)]
        for rows in q_halves:
            nc.vector.tensor_copy(q_bf[:, rows, :], q_raw[:, :, rows].rearrange("p j w -> p w j"))
        nc.vector.tensor_copy(k_sc[0:4, :], sc_picked[0:4, :].bitcast(I32))
        q_codes = sb.tile([P, NQ], U32, name="q_codes", align_bytes=64)
        q_sc = sb.tile([P, NQ], U8, name="q_sc", align_bytes=64)
        for rows in q_halves:
            nc.vector.quantize_mx(
                out=q_codes[:, rows].bitcast(FP8X4),
                scales=q_sc[:, rows],
                in_=q_bf[:, rows, :].rearrange("p w j -> p (w j)"),
            )

        kn_cols = []
        for i in range(4):
            kn_turned = ps.tile([P, P], F32, name="kn_turned%d" % i, tag="bank%d" % i)
            nc.tensor.transpose(kn_turned[:], kn_rows[i][:], ident[:])
            kn_col = sb.tile([P, 1], F32, name="kn_col%d" % i)
            nc.scalar.copy(kn_col[:], kn_turned[:, KN_ROW : KN_ROW + 1])
            kn_cols.append(kn_col)
        kn_alls = []
        for i in range(4):
            kn_spread = ps.tile([P, P], F32, name="kn_spread%d" % i)
            nc.tensor.transpose(kn_spread[:], kn_cols[i][:].to_broadcast([P, P]), ident[:])
            kn_all = sb.tile([P, P], F32, name="kn_all%d" % i, align_bytes=64)
            nc.scalar.copy(kn_all[:], kn_spread[:])
            kn_alls.append(kn_all)

        k_codes = sb.tile([P, N], U32, name="k_codes", tag="k_codes", align_bytes=64)
        dots = []
        for h in range(2):
            for j in range(2):
                cols = slice(h * HALF + j * P, h * HALF + (j + 1) * P)
                nc.vector.tensor_copy(
                    k_codes[:, cols],
                    word_tab[:].bitcast(U32).indirect(offsets[:, cols.start // 16 : cols.stop // 16]),
                )
                dot = ps.tile([P, P], F32, name="dot%d_%d" % (h, j), tag="bank%d" % (2 * h + j))
                nc.tensor.matmul_mx(
                    out=dot[:],
                    lhsT=q_codes[:].bitcast(FP8X4),
                    lhsT_scale=q_sc[:],
                    rhs=k_codes[:, cols].bitcast(FP8X4),
                    rhs_scale=k_sc[:].bitcast(U8)[:, cols],
                    start=True,
                    stop=True,
                )
                dots.append(dot)

        root = sb.tile([P, N], F32, name="root", align_bytes=64)
        parts = [sb.tile([P, P], F32, name="part%d" % i, tag="part%d" % i, align_bytes=64) for i in range(4)]
        dists = [sb.tile([P, P], F32, name="dist%d" % i, align_bytes=64) for i in range(4)]

        def add_kn(i, lo=0, hi=P):
            kn_piece = kn_alls[i][:, lo:hi]
            nc.vector.scalar_tensor_tensor(parts[i][:, lo:hi], dots[i][:, lo:hi], -2.0, kn_piece, ALU.mult, ALU.add)

        def clamp_scalar(i):
            nc.scalar.activation(dists[i][:], parts[i][:], ACT.Relu, bias=qn_col[:])

        def clamp_vector(i, lo=0, hi=P):
            nc.vector.tensor_scalar(dists[i][:, lo:hi], parts[i][:, lo:hi], qn_col[:], 0.0, ALU.add, ALU.max)

        def inv_root(i, lo=0, hi=P):
            nc.scalar.activation(
                root[:, i * P + lo : i * P + hi], dists[i][:, lo:hi], ACT.Abs_reciprocal_sqrt, bias=1.0
            )

        add_kn(0)
        add_kn(1)
        clamp_scalar(0)
        clamp_scalar(1)
        inv_root(0)
        inv_root(1)
        add_kn(2)
        add_kn(3, 0, P // 2)
        add_kn(3, P // 2, P)
        clamp_vector(2)
        inv_root(2)
        clamp_vector(3, 0, P // 2)
        clamp_vector(3, P // 2, P)
        inv_root(3, 0, P // 2)
        inv_root(3, P // 2, P)

        CUT = 2 * P
        sim0 = sb.tile([P, CUT], F32, name="sim0", tag="part3", align_bytes=64)
        total0 = sb.tile([P, 1], F32, name="total0")
        nc.vector.scalar_tensor_tensor(
            sim0[:], root[:, 0:CUT], 1.0, root[:, 0:CUT], ALU.mult, ALU.mult, accum_out=total0[:]
        )
        sim1 = sb.tile([P, N - CUT], F32, name="sim1", align_bytes=64)
        total1 = sb.tile([P, 1], F32, name="total1")
        nc.scalar.activation(sim1[:], root[:, CUT:N], ACT.Square, accum_out=total1[:])

        norm = sb.tile([P, 1], F32, name="norm")
        nc.scalar.activation(norm[:], total1[:], ACT.Abs_reciprocal_sqrt, bias=total0[:])
        res0 = sb.tile([P, CUT], F32, name="res0", align_bytes=64)
        nc.vector.tensor_scalar(res0[:], sim0[:], norm[:], norm[:], ALU.mult, ALU.mult)
        nc.sync.dma_start(out[0, :, 0:CUT], res0[:])
        res1 = sb.tile([P, N - CUT], F32, name="res1", align_bytes=64)
        nc.scalar.activation(res1[:], root[:, CUT:N], ACT.Square, scale=norm[:])
        nc.scalar.dma_start(out[0, :, CUT:N], res1[:])
